import numpy as np
import ml_dtypes


def mxq(x, axis, fmt="e4m3"):
    dtype, down = {"e4m3": (ml_dtypes.float8_e4m3fn, 7), "e5m2": (ml_dtypes.float8_e5m2, 14)}[fmt]
    v = np.moveaxis(np.asarray(x, np.float32).astype(ml_dtypes.bfloat16).astype(np.float64), axis, -1)
    blocks = v.reshape(v.shape[:-1] + (-1, 32))
    amax = np.abs(blocks).max(-1, keepdims=True)
    byte = np.maximum(np.where(amax > 0, np.frexp(amax)[1] - 1 + 127, 0) - down, 1)
    scale = np.exp2(byte - 127.0)
    codes = (blocks / scale).astype(np.float32).astype(dtype).astype(np.float64)
    return np.moveaxis((codes * scale).reshape(v.shape), -1, axis)


WIDE = False


def mx_kscale(k):
    if not WIDE:
        return np.ones(k)
    levels = np.array([10, -10, 5, -5, 0])
    if k % 512:
        return np.exp2(np.random.permutation(np.resize(levels, k // 32))).repeat(32)
    a = np.empty((k // 512, 16))
    for p in range(k // 512):
        a[p, :8] = np.random.permutation(np.resize(levels, 8))
        for g in range(8):
            far = levels[np.abs(levels - a[p, g]) >= 10]
            a[p, g + 8] = far[np.random.randint(len(far))]
    return np.exp2(a.ravel()).repeat(32)


def f64(x):
    return np.asarray(x).astype(np.float64)


def striped(idx):
    return np.tile(idx.reshape(-1, 16).T, (8, 1)).astype(np.uint16)


def unstriped(offs):
    return offs[:16].T.reshape(-1).astype(np.int64)


def pack_weight(w):
    k, n = w.shape
    w = f64(np.asarray(w, np.float32).astype(ml_dtypes.bfloat16)).reshape(k // 32, 32, n)
    amax = np.abs(w).max(1)
    byte = np.clip(np.where(amax > 0, np.frexp(amax)[1] - 1 + 127 - 7, 1), 1, 254)
    scaled = (w * np.exp2(127.0 - byte)[:, None, :]).reshape(k, n).astype(np.float32)
    words = np.ascontiguousarray(scaled.reshape(k // 512, 128, 4, n).transpose(0, 1, 3, 2)).astype(ml_dtypes.float8_e4m3fn).view(np.uint8)
    return words, np.ascontiguousarray(byte.astype(np.uint8).reshape(k // 512, 16, n))


def unpack_weight(words, scales):
    g, p, n, _ = words.shape
    vals = np.ascontiguousarray(words).view(ml_dtypes.float8_e4m3fn).astype(np.float64) * np.repeat(np.exp2(scales.astype(np.float64) - 127.0), 8, axis=1)[..., None]
    return vals.transpose(0, 1, 3, 2).reshape(g * 512, n)


K, T, S, H, V, Z, W = 512, 2048, 512, 512, 256, 512, 2048
P = 2 ** 7


def setup_inputs():
    n = np.random.standard_normal
    s = mx_kscale(K)[:, None]
    packed_xT = pack_weight(n((K, T)) * s)
    packed_eT = pack_weight(n((K, W)) * s)
    return {
        "x_words": packed_xT[0],
        "x_scales": packed_xT[1],
        "w1": (n((K, H)) / np.sqrt(K) / s).astype(np.float32),
        "w2": (n((K, H)) / np.sqrt(K) / s).astype(np.float32),
        "lam": (np.random.uniform(0.2, 0.8, (H, V))).astype(np.float32),
        "e_words": packed_eT[0],
        "e_scales": packed_eT[1],
        "unit": (np.random.uniform(0.6, 1.4, (K, 1)) / np.sqrt(K) / s).astype(np.float32),
        "tmp": (np.tile(np.random.uniform(0.6, 1.5, W), (P, 1))).astype(np.float32),
        "offs": striped(np.random.permutation(T)[:S]),
        "cra": striped(np.random.permutation(S)[:V]),
        "crb": striped(np.random.permutation(S)[:V]),
        "prt": striped(np.random.permutation(W)[:Z]),
    }


def reference(x_words, x_scales, w1, w2, lam, e_words, e_scales, unit, tmp, offs, cra, crb, prt):
    xq = unpack_weight(x_words, x_scales)[:, unstriped(offs)]
    y = mxq(f64(w1), 0, "e4m3").T @ xq
    a_ = y[:, unstriped(cra)]
    yv = mxq(f64(w2), 0, "e4m3").T @ xq
    b_ = yv[:, unstriped(crb)]
    lowr = np.minimum(a_, b_)
    mixv = f64(lam) * a_ + (-1.0 * f64(lam) + 1.0) * b_ - (0.4 * lowr)
    hid = f64(unit) * mixv
    e_prt = unpack_weight(e_words, e_scales)[:, unstriped(prt)]
    sc = mxq(hid, 0, "e4m3").T @ e_prt
    lt = sc * (f64(tmp)[:1][:, unstriped(prt)])
    mu = lt.mean(axis=1, keepdims=True)
    dl = lt - mu
    d2 = (dl) ** 2
    var_ = d2.mean(axis=1, keepdims=True)
    return dl / np.sqrt(var_ + 0.1)

@@ -1,0 +1,195 @@
+from contextlib import ExitStack
+
+import concourse.mybir as mybir
+
+F32 = mybir.dt.float32
+BF16 = mybir.dt.bfloat16
+I32 = mybir.dt.int32
+U32 = mybir.dt.uint32
+U16 = mybir.dt.uint16
+U8 = mybir.dt.uint8
+FP8X4 = mybir.dt.float8_e4m3fn_x4
+ALU = mybir.AluOpType
+ACT = mybir.ActivationFunctionType
+
+P = 128
+PACK = 4
+K = 512
+TABLE = 2048
+S = 512
+H = 512
+V = 256
+Z = 512
+EPS = 0.1
+
+FLOPS = 2 * K * H * S * 2 + 2 * H * V * Z
+BYTES = 2 * (P * TABLE * PACK + 16 * TABLE) + 2 * K * H * 4 + H * V * 4 + H * 4 + TABLE * 4 + V * Z * 4 + (S + V + V + Z) * 16
+
+
+def tile_picked_ycroplb_std_p_kernel(
+    tc, x_words, x_scales, w1, w2, lam, e_words, e_scales, unit, tmp, offs, cra, crb, prt, out
+):
+    nc = tc.nc
+    with ExitStack() as ctx:
+        keep = ctx.enter_context(tc.tile_pool(name="keep", bufs=1))
+        psum = ctx.enter_context(tc.psum_pool(name="psum", bufs=8))
+
+        def tile(name, shape, dtype):
+            return keep.tile(shape, dtype, name=name, align_bytes=64)
+
+        def load_list(name, dram, entries):
+            t = tile(name, [P, entries // 16], U16)
+            nc.sync.dma_start(t[:], dram)
+            return t
+
+        def load_words(name, dram):
+            t = tile(name, [P, TABLE], U32)
+            nc.sync.dma_start(t[:].bitcast(I32), dram[0].rearrange("p n r -> p (n r)").bitcast(I32))
+            return t
+
+        def load_scales(name, dram, clear, queue):
+            t = tile(name, [P, TABLE], U8)
+            clear.memset(t[:].bitcast(I32), 0)
+            for q in range(4):
+                queue.dma_start(t[32 * q : 32 * q + 4, :].bitcast(I32), dram[0][4 * q : 4 * q + 4, :].bitcast(I32))
+            return t
+
+        def load_weight(name, dram, c0, c1):
+            t = tile(name, [P, PACK, c1 - c0], F32)
+            nc.sync.dma_start(t[:], dram.rearrange("(p j) c -> p j c", j=PACK)[:, :, c0:c1])
+            return t
+
+        def deal(copy, grouped, raw, r0, c0, c1):
+            copy(
+                out=grouped[:].rearrange("p (t m j) -> p m t j", t=PACK, j=PACK)[:, c0 // PACK : c1 // PACK],
+                in_=raw[:, :, c0 - r0 : c1 - r0].rearrange("p j (m t) -> p m t j", t=PACK),
+            )
+
+        def gather(name, window, offsets, entries, dtype):
+            t = tile(name, [P, entries], dtype)
+            nc.vector.tensor_copy(t[:], window[:].indirect(offsets[:]))
+            return t
+
+        def product(codes, scales, c0, moving, moving_scales):
+            acc = psum.tile([P, 512], F32, name="acc")
+            nc.tensor.matmul_mx(
+                out=acc[:],
+                lhsT=codes[:, c0 : c0 + P].bitcast(FP8X4),
+                lhsT_scale=scales[:, c0 : c0 + P],
+                rhs=moving[:].bitcast(FP8X4),
+                rhs_scale=moving_scales[:],
+                start=True,
+                stop=True,
+            )
+            return acc
+
+        w2_raw = load_weight("w2_raw", w2, 0, H)
+        xs_tab = load_scales("xs_tab", x_scales, nc.vector, nc.sync)
+        offs_t = load_list("offs_t", offs, S)
+        xw_tab = load_words("xw_tab", x_words)
+        prt_t = load_list("prt_t", prt, Z)
+        w1_lo = load_weight("w1_lo", w1, 0, H // 2)
+        w1_hi = load_weight("w1_hi", w1, H // 2, H)
+        crb_t = load_list("crb_t", crb, V)
+        cra_t = load_list("cra_t", cra, V)
+        lam_t = tile("lam_t", [P, PACK, V], F32)
+        nc.sync.dma_start(lam_t[:], lam.rearrange("(p t) v -> p t v", t=PACK))
+        ew_tab = load_words("ew_tab", e_words)
+        tmp_tab = tile("tmp_tab", [P, TABLE], F32)
+        nc.sync.dma_start(tmp_tab[:], tmp)
+        es_tab = load_scales("es_tab", e_scales, nc.gpsimd, nc.gpsimd)
+        unit_t = tile("unit_t", [P, PACK], F32)
+        nc.gpsimd.dma_start(unit_t[:], unit.rearrange("(p t) o -> p (t o)", t=PACK))
+
+        xs = gather("xs", xs_tab, offs_t, S, U8)
+        w2_g = tile("w2_g", [P, H * PACK], BF16)
+        deal(nc.scalar.copy, w2_g, w2_raw, 0, 0, H // 2)
+        deal(nc.vector.tensor_copy, w2_g, w2_raw, 0, H // 2, H)
+        es = gather("es", es_tab, prt_t, Z, U8)
+        w2_c = tile("w2_c", [P, H], U32)
+        w2_s = tile("w2_s", [P, H], U8)
+        nc.vector.quantize_mx(out=w2_c[:].bitcast(FP8X4), scales=w2_s[:], in_=w2_g[:])
+        u_min = tile("u_min", [P, PACK], F32)
+        u_b = tile("u_b", [P, PACK], F32)
+        nc.vector.tensor_scalar(u_min[:], unit_t[:], -0.4, None, ALU.mult)
+        nc.vector.tensor_scalar(u_b[:], unit_t[:], 0.6, None, ALU.mult)
+        xw = gather("xw", xw_tab, offs_t, S, U32)
+
+        w1_g = tile("w1_g", [P, H * PACK], BF16)
+        deal(nc.vector.tensor_copy, w1_g, w1_lo, 0, 0, H // 2)
+        deal(nc.vector.tensor_copy, w1_g, w1_hi, H // 2, H // 2, H)
+        w1_c = tile("w1_c", [P, H], U32)
+        w1_s = tile("w1_s", [P, H], U8)
+        for c0, c1 in ((0, P), (P, H)):
+            nc.vector.quantize_mx(out=w1_c[:, c0:c1].bitcast(FP8X4), scales=w1_s[:, c0:c1], in_=w1_g[:, PACK * c0 : PACK * c1])
+        lam25 = tile("lam25", [P, PACK, V], F32)
+        nc.vector.tensor_scalar(lam25[:], lam_t[:], 2.5, None, ALU.mult)
+
+        acc_v = [product(w2_c, w2_s, P * t, xw, xs) for t in range(PACK)]
+        acc_y = [product(w1_c, w1_s, P * t, xw, xs) for t in range(PACK)]
+        yv = [tile("yv%d" % t, [P, S], F32) for t in range(PACK)]
+        y = [tile("y%d" % t, [P, S], F32) for t in range(PACK)]
+        b = [tile("b%d" % t, [P, V], F32) for t in range(PACK)]
+        d = [tile("d%d" % t, [P, V], F32) for t in range(PACK)]
+        coef = [tile("coef%d" % t, [P, V], F32) for t in range(PACK)]
+        term = [tile("term%d" % t, [P, V], F32) for t in range(PACK)]
+        hid = tile("hid", [P, PACK, V], F32)
+
+        def fetch_b(t):
+            nc.scalar.activation(b[t][:], yv[t][:].indirect(crb_t[:]), ACT.Copy)
+
+        nc.scalar.copy(yv[0][:], acc_v[0][:])
+        nc.scalar.copy(yv[1][:], acc_v[1][:])
+        fetch_b(0)
+        fetch_b(1)
+        nc.vector.tensor_copy(y[0][:], acc_y[0][:])
+        for t in range(1, PACK):
+            if t + 1 < PACK:
+                nc.scalar.copy(yv[t + 1][:], acc_v[t + 1][:])
+            nc.scalar.copy(y[t][:], acc_y[t][:])
+            if t + 1 < PACK:
+                fetch_b(t + 1)
+
+        ew = gather("ew", ew_tab, prt_t, Z, U32)
+        for s in range(PACK + 1):
+            if s < PACK:
+                nc.vector.tensor_tensor(d[s][:], y[s][:].indirect(cra_t[:]), b[s][:], ALU.subtract)
+            if s > 0:
+                nc.vector.scalar_tensor_tensor(term[s - 1][:], coef[s - 1][:], u_min[:, s - 1 : s], d[s - 1][:], ALU.mult, ALU.mult)
+            if s < PACK:
+                nc.vector.scalar_tensor_tensor(coef[s][:], d[s][:], 0.0, lam25[:, s, :], ALU.is_lt, ALU.subtract)
+            if s > 0:
+                nc.vector.scalar_tensor_tensor(hid[:, s - 1, :], b[s - 1][:], u_b[:, s - 1 : s], term[s - 1][:], ALU.mult, ALU.add)
+
+        temp = tile("temp", [P, Z], F32)
+        nc.scalar.activation(temp[:], tmp_tab[:].indirect(prt_t[:]), ACT.Copy)
+
+        halves = range(V // P)
+        hid_g = [tile("hid_g%d" % h, [P, P, PACK], BF16) for h in halves]
+        hid_c = [tile("hid_c%d" % h, [P, P], U32) for h in halves]
+        hid_s = [tile("hid_s%d" % h, [P, P], U8) for h in halves]
+        for h, copy in zip(halves, (nc.vector.tensor_copy, nc.scalar.copy)):
+            copy(out=hid_g[h][:], in_=hid[:, :, P * h : P * (h + 1)].rearrange("p t v -> p v t"))
+        acc_s = []
+        for h in halves:
+            nc.vector.quantize_mx(out=hid_c[h][:].bitcast(FP8X4), scales=hid_s[h][:], in_=hid_g[h][:].rearrange("p v t -> p (v t)"))
+            acc_s.append(product(hid_c[h], hid_s[h], 0, ew, es))
+
+        part = [tile("part%d" % h, [P, Z], F32) for h in halves]
+        mu = [tile("mu%d" % h, [P, 1], F32) for h in halves]
+        mu_part = [tile("mu_part%d" % h, [P, 1], F32) for h in halves]
+        sq = [tile("sq%d" % h, [P, Z], F32) for h in halves]
+        ssq = [tile("ssq%d" % h, [P, 1], F32) for h in halves]
+        dev = [tile("dev%d" % h, [P, 1], F32) for h in halves]
+        inv = [tile("inv%d" % h, [P, 1], F32) for h in halves]
+        res = [tile("res%d" % h, [P, Z], F32) for h in halves]
+        for h in halves:
+            nc.vector.scalar_tensor_tensor(part[h][:], acc_s[h][:], 1.0 / Z, temp[:], ALU.mult, ALU.mult, accum_out=mu[h][:])
+            nc.scalar.activation(sq[h][:], part[h][:], ACT.Square, bias=mu[h][:], scale=-float(Z), accum_out=ssq[h][:])
+            nc.scalar.activation(dev[h][:], ssq[h][:], ACT.Sqrt, bias=EPS / Z**2, scale=1.0 / Z**3)
+        for h in halves:
+            nc.vector.tensor_scalar(mu_part[h][:], mu[h][:], 1.0 / Z, None, ALU.mult)
+        for h in halves:
+            nc.vector.reciprocal(inv[h][:], dev[h][:])
+            nc.vector.tensor_scalar(res[h][:], part[h][:], mu_part[h][:], inv[h][:], ALU.subtract, ALU.mult)
+            nc.sync.dma_start(out[P * h : P * (h + 1), :], res[h][:])

@@ -47,11 +47,11 @@ def tile_picked_ycroplb_std_p_kernel(
             nc.sync.dma_start(t[:].bitcast(I32), dram[0].rearrange("p n r -> p (n r)").bitcast(I32))
             return t
 
-        def load_scales(name, dram, clear, queue):
+        def load_scales(name, dram):
             t = tile(name, [P, TABLE], U8)
-            clear.memset(t[:].bitcast(I32), 0)
-            for q in range(4):
-                queue.dma_start(t[32 * q : 32 * q + 4, :].bitcast(I32), dram[0][4 * q : 4 * q + 4, :].bitcast(I32))
+            rows = dram[0].bitcast(I32).rearrange("(q r) n -> r q n", r=4)
+            for r in range(4):
+                nc.sync.dma_start(t[r:P:4, :].bitcast(I32), rows[r].unsqueeze(1).to_broadcast([4, 8, TABLE // 4]))
             return t
 
         def load_weight(name, dram, c0, c1):
@@ -83,23 +83,28 @@ def tile_picked_ycroplb_std_p_kernel(
             )
             return acc
 
-        w2_raw = load_weight("w2_raw", w2, 0, H)
-        xs_tab = load_scales("xs_tab", x_scales, nc.vector, nc.sync)
         offs_t = load_list("offs_t", offs, S)
-        xw_tab = load_words("xw_tab", x_words)
+        xs_tab = load_scales("xs_tab", x_scales)
+        w2_raw = load_weight("w2_raw", w2, 0, H)
         prt_t = load_list("prt_t", prt, Z)
+        es_tab = load_scales("es_tab", e_scales)
+        xw_tab = load_words("xw_tab", x_words)
+        crb_t = load_list("crb_t", crb, V)
         w1_lo = load_weight("w1_lo", w1, 0, H // 2)
         w1_hi = load_weight("w1_hi", w1, H // 2, H)
-        crb_t = load_list("crb_t", crb, V)
         cra_t = load_list("cra_t", cra, V)
+        unit_t = tile("unit_t", [P, PACK], F32)
+        nc.sync.dma_start(unit_t[:], unit.rearrange("(p t) o -> p (t o)", t=PACK))
         lam_t = tile("lam_t", [P, PACK, V], F32)
         nc.sync.dma_start(lam_t[:], lam.rearrange("(p t) v -> p t v", t=PACK))
         ew_tab = load_words("ew_tab", e_words)
         tmp_tab = tile("tmp_tab", [P, TABLE], F32)
         nc.sync.dma_start(tmp_tab[:], tmp)
-        es_tab = load_scales("es_tab", e_scales, nc.gpsimd, nc.gpsimd)
-        unit_t = tile("unit_t", [P, PACK], F32)
-        nc.gpsimd.dma_start(unit_t[:], unit.rearrange("(p t) o -> p (t o)", t=PACK))
+
+        warm = tile("warm", [P, 1], F32)
+        warm_out = tile("warm_out", [P, 1], F32)
+        nc.gpsimd.memset(warm[:], 1.0)
+        nc.scalar.activation(warm_out[:], warm[:], ACT.Abs_reciprocal_sqrt)
 
         xs = gather("xs", xs_tab, offs_t, S, U8)
         w2_g = tile("w2_g", [P, H * PACK], BF16)
@@ -180,16 +185,14 @@ def tile_picked_ycroplb_std_p_kernel(
         mu_part = [tile("mu_part%d" % h, [P, 1], F32) for h in halves]
         sq = [tile("sq%d" % h, [P, Z], F32) for h in halves]
         ssq = [tile("ssq%d" % h, [P, 1], F32) for h in halves]
-        dev = [tile("dev%d" % h, [P, 1], F32) for h in halves]
         inv = [tile("inv%d" % h, [P, 1], F32) for h in halves]
         res = [tile("res%d" % h, [P, Z], F32) for h in halves]
         for h in halves:
             nc.vector.scalar_tensor_tensor(part[h][:], acc_s[h][:], 1.0 / Z, temp[:], ALU.mult, ALU.mult, accum_out=mu[h][:])
             nc.scalar.activation(sq[h][:], part[h][:], ACT.Square, bias=mu[h][:], scale=-float(Z), accum_out=ssq[h][:])
-            nc.scalar.activation(dev[h][:], ssq[h][:], ACT.Sqrt, bias=EPS / Z**2, scale=1.0 / Z**3)
+            nc.scalar.activation(inv[h][:], ssq[h][:], ACT.Abs_reciprocal_sqrt, bias=EPS / Z**2, scale=1.0 / Z**3)
         for h in halves:
             nc.vector.tensor_scalar(mu_part[h][:], mu[h][:], 1.0 / Z, None, ALU.mult)
         for h in halves:
-            nc.vector.reciprocal(inv[h][:], dev[h][:])
             nc.vector.tensor_scalar(res[h][:], part[h][:], mu_part[h][:], inv[h][:], ALU.subtract, ALU.mult)
             nc.sync.dma_start(out[P * h : P * (h + 1), :], res[h][:])

@@ -49,9 +49,9 @@ def tile_picked_ycroplb_std_p_kernel(
 
         def load_scales(name, dram):
             t = tile(name, [P, TABLE], U8)
-            rows = dram[0].bitcast(I32).rearrange("(q r) n -> r q n", r=4)
-            for r in range(4):
-                nc.sync.dma_start(t[r:P:4, :].bitcast(I32), rows[r].unsqueeze(1).to_broadcast([4, 8, TABLE // 4]))
+            nc.vector.memset(t[:].bitcast(I32), 0)
+            for q in range(4):
+                nc.gpsimd.dma_start(t[32 * q : 32 * q + 4, :].bitcast(I32), dram[0][4 * q : 4 * q + 4, :].bitcast(I32))
             return t
 
         def load_weight(name, dram, c0, c1):
@@ -83,20 +83,20 @@ def tile_picked_ycroplb_std_p_kernel(
             )
             return acc
 
-        offs_t = load_list("offs_t", offs, S)
         xs_tab = load_scales("xs_tab", x_scales)
-        w2_raw = load_weight("w2_raw", w2, 0, H)
-        prt_t = load_list("prt_t", prt, Z)
         es_tab = load_scales("es_tab", e_scales)
+        w2_raw = load_weight("w2_raw", w2, 0, H)
+        offs_t = load_list("offs_t", offs, S)
         xw_tab = load_words("xw_tab", x_words)
-        crb_t = load_list("crb_t", crb, V)
         w1_lo = load_weight("w1_lo", w1, 0, H // 2)
         w1_hi = load_weight("w1_hi", w1, H // 2, H)
+        crb_t = load_list("crb_t", crb, V)
         cra_t = load_list("cra_t", cra, V)
-        unit_t = tile("unit_t", [P, PACK], F32)
-        nc.sync.dma_start(unit_t[:], unit.rearrange("(p t) o -> p (t o)", t=PACK))
+        prt_t = load_list("prt_t", prt, Z)
         lam_t = tile("lam_t", [P, PACK, V], F32)
         nc.sync.dma_start(lam_t[:], lam.rearrange("(p t) v -> p t v", t=PACK))
+        unit_t = tile("unit_t", [P, PACK], F32)
+        nc.sync.dma_start(unit_t[:], unit.rearrange("(p t) o -> p (t o)", t=PACK))
         ew_tab = load_words("ew_tab", e_words)
         tmp_tab = tile("tmp_tab", [P, TABLE], F32)
         nc.sync.dma_start(tmp_tab[:], tmp)
@@ -106,18 +106,13 @@ def tile_picked_ycroplb_std_p_kernel(
         nc.gpsimd.memset(warm[:], 1.0)
         nc.scalar.activation(warm_out[:], warm[:], ACT.Abs_reciprocal_sqrt)
 
-        xs = gather("xs", xs_tab, offs_t, S, U8)
         w2_g = tile("w2_g", [P, H * PACK], BF16)
         deal(nc.scalar.copy, w2_g, w2_raw, 0, 0, H // 2)
         deal(nc.vector.tensor_copy, w2_g, w2_raw, 0, H // 2, H)
-        es = gather("es", es_tab, prt_t, Z, U8)
+        xs = gather("xs", xs_tab, offs_t, S, U8)
         w2_c = tile("w2_c", [P, H], U32)
         w2_s = tile("w2_s", [P, H], U8)
         nc.vector.quantize_mx(out=w2_c[:].bitcast(FP8X4), scales=w2_s[:], in_=w2_g[:])
-        u_min = tile("u_min", [P, PACK], F32)
-        u_b = tile("u_b", [P, PACK], F32)
-        nc.vector.tensor_scalar(u_min[:], unit_t[:], -0.4, None, ALU.mult)
-        nc.vector.tensor_scalar(u_b[:], unit_t[:], 0.6, None, ALU.mult)
         xw = gather("xw", xw_tab, offs_t, S, U32)
 
         w1_g = tile("w1_g", [P, H * PACK], BF16)
@@ -128,7 +123,13 @@ def tile_picked_ycroplb_std_p_kernel(
         for c0, c1 in ((0, P), (P, H)):
             nc.vector.quantize_mx(out=w1_c[:, c0:c1].bitcast(FP8X4), scales=w1_s[:, c0:c1], in_=w1_g[:, PACK * c0 : PACK * c1])
         lam25 = tile("lam25", [P, PACK, V], F32)
-        nc.vector.tensor_scalar(lam25[:], lam_t[:], 2.5, None, ALU.mult)
+        es = gather("es", es_tab, prt_t, Z, U8)
+        for t in range(PACK):
+            nc.gpsimd.tensor_scalar(lam25[:, t, :], lam_t[:, t, :], 2.5, 0.0, ALU.mult, ALU.add)
+        u_min = tile("u_min", [P, PACK], F32)
+        u_b = tile("u_b", [P, PACK], F32)
+        nc.gpsimd.tensor_scalar(u_min[:], unit_t[:], -0.4, 0.0, ALU.mult, ALU.add)
+        nc.gpsimd.tensor_scalar(u_b[:], unit_t[:], 0.6, 0.0, ALU.mult, ALU.add)
 
         acc_v = [product(w2_c, w2_s, P * t, xw, xs) for t in range(PACK)]
         acc_y = [product(w1_c, w1_s, P * t, xw, xs) for t in range(PACK)]
@@ -144,16 +145,11 @@ def tile_picked_ycroplb_std_p_kernel(
             nc.scalar.activation(b[t][:], yv[t][:].indirect(crb_t[:]), ACT.Copy)
 
         nc.scalar.copy(yv[0][:], acc_v[0][:])
-        nc.scalar.copy(yv[1][:], acc_v[1][:])
-        fetch_b(0)
-        fetch_b(1)
-        nc.vector.tensor_copy(y[0][:], acc_y[0][:])
-        for t in range(1, PACK):
+        for t in range(PACK):
             if t + 1 < PACK:
                 nc.scalar.copy(yv[t + 1][:], acc_v[t + 1][:])
+            fetch_b(t)
             nc.scalar.copy(y[t][:], acc_y[t][:])
-            if t + 1 < PACK:
-                fetch_b(t + 1)
 
         ew = gather("ew", ew_tab, prt_t, Z, U32)
         for s in range(PACK + 1):
@@ -166,7 +162,7 @@ def tile_picked_ycroplb_std_p_kernel(
             if s > 0:
                 nc.vector.scalar_tensor_tensor(hid[:, s - 1, :], b[s - 1][:], u_b[:, s - 1 : s], term[s - 1][:], ALU.mult, ALU.add)
 
-        temp = tile("temp", [P, Z], F32)
+        temp = tile("yv%d" % (PACK - 1), [P, Z], F32)
         nc.scalar.activation(temp[:], tmp_tab[:].indirect(prt_t[:]), ACT.Copy)
 
         halves = range(V // P)

@@ -32,7 +32,9 @@ def tile_picked_ycroplb_std_p_kernel(
     nc = tc.nc
     with ExitStack() as ctx:
         keep = ctx.enter_context(tc.tile_pool(name="keep", bufs=1))
-        psum = ctx.enter_context(tc.psum_pool(name="psum", bufs=8))
+        shared = ctx.enter_context(tc.tile_pool(name="shared", bufs=1))
+        late = ctx.enter_context(tc.tile_pool(name="late", bufs=1))
+        psum = ctx.enter_context(tc.psum_pool(name="psum", bufs=1))
 
         def tile(name, shape, dtype):
             return keep.tile(shape, dtype, name=name, align_bytes=64)
@@ -42,20 +44,25 @@ def tile_picked_ycroplb_std_p_kernel(
             nc.sync.dma_start(t[:], dram)
             return t
 
-        def load_words(name, dram):
+        def load_words(name, dram, pieces):
             t = tile(name, [P, TABLE], U32)
-            nc.sync.dma_start(t[:].bitcast(I32), dram[0].rearrange("p n r -> p (n r)").bitcast(I32))
+            words = dram[0].rearrange("p n r -> p (n r)").bitcast(I32)
+            width = TABLE // pieces
+            for c0 in range(0, TABLE, width):
+                nc.sync.dma_start(t[:, c0 : c0 + width].bitcast(I32), words[:, c0 : c0 + width])
             return t
 
-        def load_scales(name, dram):
-            t = tile(name, [P, TABLE], U8)
-            nc.vector.memset(t[:].bitcast(I32), 0)
+        def load_scales(t, dram, clears):
+            words = t[:].bitcast(I32)
+            share = TABLE // 4 // len(clears)
+            for n, engine in enumerate(clears):
+                engine.memset(words[:, n * share : (n + 1) * share], 0)
             for q in range(4):
-                nc.gpsimd.dma_start(t[32 * q : 32 * q + 4, :].bitcast(I32), dram[0][4 * q : 4 * q + 4, :].bitcast(I32))
+                nc.sync.dma_start(t[32 * q : 32 * q + 4, :].bitcast(I32), dram[0][4 * q : 4 * q + 4, :].bitcast(I32))
             return t
 
         def load_weight(name, dram, c0, c1):
-            t = tile(name, [P, PACK, c1 - c0], F32)
+            t = shared.tile([P, PACK, c1 - c0], F32, name=name, offset=c0 * PACK * 4)
             nc.sync.dma_start(t[:], dram.rearrange("(p j) c -> p j c", j=PACK)[:, :, c0:c1])
             return t
 
@@ -70,8 +77,8 @@ def tile_picked_ycroplb_std_p_kernel(
             nc.vector.tensor_copy(t[:], window[:].indirect(offsets[:]))
             return t
 
-        def product(codes, scales, c0, moving, moving_scales):
-            acc = psum.tile([P, 512], F32, name="acc")
+        def product(bank, codes, scales, c0, moving, moving_scales):
+            acc = psum.tile([P, 512], F32, name="bank%d" % bank)
             nc.tensor.matmul_mx(
                 out=acc[:],
                 lhsT=codes[:, c0 : c0 + P].bitcast(FP8X4),
@@ -83,21 +90,24 @@ def tile_picked_ycroplb_std_p_kernel(
             )
             return acc
 
-        xs_tab = load_scales("xs_tab", x_scales)
-        es_tab = load_scales("es_tab", e_scales)
-        w2_raw = load_weight("w2_raw", w2, 0, H)
         offs_t = load_list("offs_t", offs, S)
-        xw_tab = load_words("xw_tab", x_words)
+        w2_raw = tile("w2_raw", [P, PACK, H], F32)
+        w2_rows = w2.rearrange("(p j) c -> p j c", j=PACK)
+        for j0, j1 in ((0, 1), (1, 2), (2, 4)):
+            nc.sync.dma_start(w2_raw[:, j0:j1, :], w2_rows[:, j0:j1, :])
+        xw_tab = load_words("xw_tab", x_words, 4)
+        xs_tab = load_scales(tile("xs_tab", [P, TABLE], U8), x_scales, (nc.vector, nc.gpsimd))
         w1_lo = load_weight("w1_lo", w1, 0, H // 2)
         w1_hi = load_weight("w1_hi", w1, H // 2, H)
         crb_t = load_list("crb_t", crb, V)
-        cra_t = load_list("cra_t", cra, V)
-        prt_t = load_list("prt_t", prt, Z)
         lam_t = tile("lam_t", [P, PACK, V], F32)
         nc.sync.dma_start(lam_t[:], lam.rearrange("(p t) v -> p t v", t=PACK))
+        prt_t = load_list("prt_t", prt, Z)
+        es_tab = load_scales(tile("es_tab", [P, TABLE], U8), e_scales, (nc.vector,))
+        cra_t = load_list("cra_t", cra, V)
+        ew_tab = load_words("ew_tab", e_words, 1)
         unit_t = tile("unit_t", [P, PACK], F32)
         nc.sync.dma_start(unit_t[:], unit.rearrange("(p t) o -> p (t o)", t=PACK))
-        ew_tab = load_words("ew_tab", e_words)
         tmp_tab = tile("tmp_tab", [P, TABLE], F32)
         nc.sync.dma_start(tmp_tab[:], tmp)
 
@@ -109,34 +119,33 @@ def tile_picked_ycroplb_std_p_kernel(
         w2_g = tile("w2_g", [P, H * PACK], BF16)
         deal(nc.scalar.copy, w2_g, w2_raw, 0, 0, H // 2)
         deal(nc.vector.tensor_copy, w2_g, w2_raw, 0, H // 2, H)
-        xs = gather("xs", xs_tab, offs_t, S, U8)
         w2_c = tile("w2_c", [P, H], U32)
         w2_s = tile("w2_s", [P, H], U8)
         nc.vector.quantize_mx(out=w2_c[:].bitcast(FP8X4), scales=w2_s[:], in_=w2_g[:])
         xw = gather("xw", xw_tab, offs_t, S, U32)
+        xs = gather("xs", xs_tab, offs_t, S, U8)
 
-        w1_g = tile("w1_g", [P, H * PACK], BF16)
-        deal(nc.vector.tensor_copy, w1_g, w1_lo, 0, 0, H // 2)
+        w1_g = late.tile([P, H * PACK], BF16, name="w1_g", offset=0, align_bytes=64)
+        deal(nc.scalar.copy, w1_g, w1_lo, 0, 0, H // 2)
         deal(nc.vector.tensor_copy, w1_g, w1_hi, H // 2, H // 2, H)
         w1_c = tile("w1_c", [P, H], U32)
         w1_s = tile("w1_s", [P, H], U8)
         for c0, c1 in ((0, P), (P, H)):
             nc.vector.quantize_mx(out=w1_c[:, c0:c1].bitcast(FP8X4), scales=w1_s[:, c0:c1], in_=w1_g[:, PACK * c0 : PACK * c1])
-        lam25 = tile("lam25", [P, PACK, V], F32)
-        es = gather("es", es_tab, prt_t, Z, U8)
-        for t in range(PACK):
-            nc.gpsimd.tensor_scalar(lam25[:, t, :], lam_t[:, t, :], 2.5, 0.0, ALU.mult, ALU.add)
+        lam25 = late.tile([P, PACK, V], F32, name="lam25", offset=Z, align_bytes=64)
+        nc.vector.tensor_scalar(lam25[:], lam_t[:], 2.5, None, ALU.mult)
+        es = late.tile([P, Z], U8, name="es", offset=0, align_bytes=64)
+        nc.vector.tensor_copy(es[:], es_tab[:].indirect(prt_t[:]))
         u_min = tile("u_min", [P, PACK], F32)
         u_b = tile("u_b", [P, PACK], F32)
         nc.gpsimd.tensor_scalar(u_min[:], unit_t[:], -0.4, 0.0, ALU.mult, ALU.add)
         nc.gpsimd.tensor_scalar(u_b[:], unit_t[:], 0.6, 0.0, ALU.mult, ALU.add)
 
-        acc_v = [product(w2_c, w2_s, P * t, xw, xs) for t in range(PACK)]
-        acc_y = [product(w1_c, w1_s, P * t, xw, xs) for t in range(PACK)]
-        yv = [tile("yv%d" % t, [P, S], F32) for t in range(PACK)]
+        yv = [shared.tile([P, S], F32, name="yv%d" % t, offset=t * S * 4) for t in range(PACK)]
         y = [tile("y%d" % t, [P, S], F32) for t in range(PACK)]
         b = [tile("b%d" % t, [P, V], F32) for t in range(PACK)]
-        d = [tile("d%d" % t, [P, V], F32) for t in range(PACK)]
+        d = [tile("es_tab", [P, V], F32), tile("d1", [P, V], F32)]
+        a = {t: tile("a%d" % t, [P, V], F32) for t in (2, 3)}
         coef = [tile("coef%d" % t, [P, V], F32) for t in range(PACK)]
         term = [tile("term%d" % t, [P, V], F32) for t in range(PACK)]
         hid = tile("hid", [P, PACK, V], F32)
@@ -144,25 +153,53 @@ def tile_picked_ycroplb_std_p_kernel(
         def fetch_b(t):
             nc.scalar.activation(b[t][:], yv[t][:].indirect(crb_t[:]), ACT.Copy)
 
-        nc.scalar.copy(yv[0][:], acc_v[0][:])
-        for t in range(PACK):
-            if t + 1 < PACK:
-                nc.scalar.copy(yv[t + 1][:], acc_v[t + 1][:])
+        def fetch_a(t):
+            nc.scalar.activation(a[t][:], y[t][:].indirect(cra_t[:]), ACT.Copy)
+
+        acc_v = [product(t, w2_c, w2_s, P * t, xw, xs) for t in range(2)]
+        acc_y = [product(2 + t, w1_c, w1_s, P * t, xw, xs) for t in range(PACK)]
+        for t in range(2):
+            nc.scalar.copy(yv[t][:], acc_v[t][:])
+        for t in range(2):
             fetch_b(t)
             nc.scalar.copy(y[t][:], acc_y[t][:])
+        for t in range(2, PACK):
+            nc.scalar.copy(yv[t][:], product(t, w2_c, w2_s, P * t, xw, xs)[:])
+            nc.scalar.copy(y[t][:], acc_y[t][:])
+            fetch_b(t)
+            fetch_a(t)
 
-        ew = gather("ew", ew_tab, prt_t, Z, U32)
-        for s in range(PACK + 1):
-            if s < PACK:
-                nc.vector.tensor_tensor(d[s][:], y[s][:].indirect(cra_t[:]), b[s][:], ALU.subtract)
-            if s > 0:
-                nc.vector.scalar_tensor_tensor(term[s - 1][:], coef[s - 1][:], u_min[:, s - 1 : s], d[s - 1][:], ALU.mult, ALU.mult)
-            if s < PACK:
-                nc.vector.scalar_tensor_tensor(coef[s][:], d[s][:], 0.0, lam25[:, s, :], ALU.is_lt, ALU.subtract)
-            if s > 0:
-                nc.vector.scalar_tensor_tensor(hid[:, s - 1, :], b[s - 1][:], u_b[:, s - 1 : s], term[s - 1][:], ALU.mult, ALU.add)
+        def share(t, v0, v1):
+            nc.vector.scalar_tensor_tensor(coef[t][:, v0:v1], d[t][:, v0:v1], 0.0, lam25[:, t, v0:v1], ALU.is_lt, ALU.subtract)
 
-        temp = tile("yv%d" % (PACK - 1), [P, Z], F32)
+        def scale(t, v0, v1):
+            nc.vector.scalar_tensor_tensor(term[t][:, v0:v1], coef[t][:, v0:v1], u_min[:, t : t + 1], d[t][:, v0:v1], ALU.mult, ALU.mult)
+
+        def join(t, v0, v1):
+            nc.vector.scalar_tensor_tensor(hid[:, t, v0:v1], b[t][:, v0:v1], u_b[:, t : t + 1], term[t][:, v0:v1], ALU.mult, ALU.add)
+
+        for t in range(2):
+            nc.vector.tensor_tensor(d[t][:], y[t][:].indirect(cra_t[:]), b[t][:], ALU.subtract)
+        share(0, 0, V)
+        share(1, 0, V)
+        ew = gather("y1", ew_tab, prt_t, Z, U32)
+        scale(0, 0, V)
+        scale(1, 0, V)
+        join(0, 0, V)
+        d.append(tile("ew_tab", [P, V], F32))
+        nc.vector.tensor_tensor(d[2][:], a[2][:], b[2][:], ALU.subtract)
+        join(1, 0, V)
+        share(2, 0, V)
+        d.append(tile("term0", [P, V], F32))
+        nc.vector.tensor_tensor(d[3][:], a[3][:], b[3][:], ALU.subtract)
+        scale(2, 0, V)
+        share(3, 0, V)
+        join(2, 0, V)
+        for step in (scale, join):
+            for v0 in range(0, V, P):
+                step(3, v0, v0 + P)
+
+        temp = tile("y3", [P, Z], F32)
         nc.scalar.activation(temp[:], tmp_tab[:].indirect(prt_t[:]), ACT.Copy)
 
         halves = range(V // P)
@@ -174,7 +211,7 @@ def tile_picked_ycroplb_std_p_kernel(
         acc_s = []
         for h in halves:
             nc.vector.quantize_mx(out=hid_c[h][:].bitcast(FP8X4), scales=hid_s[h][:], in_=hid_g[h][:].rearrange("p v t -> p (v t)"))
-            acc_s.append(product(hid_c[h], hid_s[h], 0, ew, es))
+            acc_s.append(product(6 + h, hid_c[h], hid_s[h], 0, ew, es))
 
         part = [tile("part%d" % h, [P, Z], F32) for h in halves]
         mu = [tile("mu%d" % h, [P, 1], F32) for h in halves]
@@ -186,6 +223,7 @@ def tile_picked_ycroplb_std_p_kernel(
         for h in halves:
             nc.vector.scalar_tensor_tensor(part[h][:], acc_s[h][:], 1.0 / Z, temp[:], ALU.mult, ALU.mult, accum_out=mu[h][:])
             nc.scalar.activation(sq[h][:], part[h][:], ACT.Square, bias=mu[h][:], scale=-float(Z), accum_out=ssq[h][:])
+        for h in halves:
             nc.scalar.activation(inv[h][:], ssq[h][:], ACT.Abs_reciprocal_sqrt, bias=EPS / Z**2, scale=1.0 / Z**3)
         for h in halves:
             nc.vector.tensor_scalar(mu_part[h][:], mu[h][:], 1.0 / Z, None, ALU.mult)

from contextlib import ExitStack

import concourse.mybir as mybir

F32 = mybir.dt.float32
BF16 = mybir.dt.bfloat16
I32 = mybir.dt.int32
U32 = mybir.dt.uint32
U16 = mybir.dt.uint16
U8 = mybir.dt.uint8
FP8X4 = mybir.dt.float8_e4m3fn_x4
ALU = mybir.AluOpType
ACT = mybir.ActivationFunctionType

P = 128
PACK = 4
K = 512
TABLE = 2048
S = 512
H = 512
V = 256
Z = 512
EPS = 0.1

FLOPS = 2 * K * H * S * 2 + 2 * H * V * Z
BYTES = 2 * (P * TABLE * PACK + 16 * TABLE) + 2 * K * H * 4 + H * V * 4 + H * 4 + TABLE * 4 + V * Z * 4 + (S + V + V + Z) * 16


def tile_picked_ycroplb_std_p_kernel(
    tc, x_words, x_scales, w1, w2, lam, e_words, e_scales, unit, tmp, offs, cra, crb, prt, out
):
    nc = tc.nc
    with ExitStack() as ctx:
        keep = ctx.enter_context(tc.tile_pool(name="keep", bufs=1))
        shared = ctx.enter_context(tc.tile_pool(name="shared", bufs=1))
        late = ctx.enter_context(tc.tile_pool(name="late", bufs=1))
        psum = ctx.enter_context(tc.psum_pool(name="psum", bufs=1))

        def tile(name, shape, dtype):
            return keep.tile(shape, dtype, name=name, align_bytes=64)

        def load_list(name, dram, entries):
            t = tile(name, [P, entries // 16], U16)
            nc.sync.dma_start(t[:], dram)
            return t

        def load_words(name, dram, pieces):
            t = tile(name, [P, TABLE], U32)
            words = dram[0].rearrange("p n r -> p (n r)").bitcast(I32)
            width = TABLE // pieces
            for c0 in range(0, TABLE, width):
                nc.sync.dma_start(t[:, c0 : c0 + width].bitcast(I32), words[:, c0 : c0 + width])
            return t

        def load_scales(t, dram, clears):
            words = t[:].bitcast(I32)
            share = TABLE // 4 // len(clears)
            for n, engine in enumerate(clears):
                engine.memset(words[:, n * share : (n + 1) * share], 0)
            for q in range(4):
                nc.sync.dma_start(t[32 * q : 32 * q + 4, :].bitcast(I32), dram[0][4 * q : 4 * q + 4, :].bitcast(I32))
            return t

        def load_weight(name, dram, c0, c1):
            t = shared.tile([P, PACK, c1 - c0], F32, name=name, offset=c0 * PACK * 4)
            nc.sync.dma_start(t[:], dram.rearrange("(p j) c -> p j c", j=PACK)[:, :, c0:c1])
            return t

        def deal(copy, grouped, raw, r0, c0, c1):
            copy(
                out=grouped[:].rearrange("p (t m j) -> p m t j", t=PACK, j=PACK)[:, c0 // PACK : c1 // PACK],
                in_=raw[:, :, c0 - r0 : c1 - r0].rearrange("p j (m t) -> p m t j", t=PACK),
            )

        def gather(name, window, offsets, entries, dtype):
            t = tile(name, [P, entries], dtype)
            nc.vector.tensor_copy(t[:], window[:].indirect(offsets[:]))
            return t

        def product(bank, codes, scales, c0, moving, moving_scales):
            acc = psum.tile([P, 512], F32, name="bank%d" % bank)
            nc.tensor.matmul_mx(
                out=acc[:],
                lhsT=codes[:, c0 : c0 + P].bitcast(FP8X4),
                lhsT_scale=scales[:, c0 : c0 + P],
                rhs=moving[:].bitcast(FP8X4),
                rhs_scale=moving_scales[:],
                start=True,
                stop=True,
            )
            return acc

        offs_t = load_list("offs_t", offs, S)
        w2_raw = tile("w2_raw", [P, PACK, H], F32)
        w2_rows = w2.rearrange("(p j) c -> p j c", j=PACK)
        for j0, j1 in ((0, 1), (1, 2), (2, 4)):
            nc.sync.dma_start(w2_raw[:, j0:j1, :], w2_rows[:, j0:j1, :])
        xw_tab = load_words("xw_tab", x_words, 4)
        xs_tab = load_scales(tile("xs_tab", [P, TABLE], U8), x_scales, (nc.vector, nc.gpsimd))
        w1_lo = load_weight("w1_lo", w1, 0, H // 2)
        w1_hi = load_weight("w1_hi", w1, H // 2, H)
        crb_t = load_list("crb_t", crb, V)
        lam_t = tile("lam_t", [P, PACK, V], F32)
        nc.sync.dma_start(lam_t[:], lam.rearrange("(p t) v -> p t v", t=PACK))
        prt_t = load_list("prt_t", prt, Z)
        es_tab = load_scales(tile("es_tab", [P, TABLE], U8), e_scales, (nc.vector,))
        cra_t = load_list("cra_t", cra, V)
        ew_tab = load_words("ew_tab", e_words, 1)
        unit_t = tile("unit_t", [P, PACK], F32)
        nc.sync.dma_start(unit_t[:], unit.rearrange("(p t) o -> p (t o)", t=PACK))
        tmp_tab = tile("tmp_tab", [P, TABLE], F32)
        nc.sync.dma_start(tmp_tab[:], tmp)

        warm = tile("warm", [P, 1], F32)
        warm_out = tile("warm_out", [P, 1], F32)
        nc.gpsimd.memset(warm[:], 1.0)
        nc.scalar.activation(warm_out[:], warm[:], ACT.Abs_reciprocal_sqrt)

        w2_g = tile("w2_g", [P, H * PACK], BF16)
        deal(nc.scalar.copy, w2_g, w2_raw, 0, 0, H // 2)
        deal(nc.vector.tensor_copy, w2_g, w2_raw, 0, H // 2, H)
        w2_c = tile("w2_c", [P, H], U32)
        w2_s = tile("w2_s", [P, H], U8)
        nc.vector.quantize_mx(out=w2_c[:].bitcast(FP8X4), scales=w2_s[:], in_=w2_g[:])
        xw = gather("xw", xw_tab, offs_t, S, U32)
        xs = gather("xs", xs_tab, offs_t, S, U8)

        w1_g = late.tile([P, H * PACK], BF16, name="w1_g", offset=0, align_bytes=64)
        deal(nc.scalar.copy, w1_g, w1_lo, 0, 0, H // 2)
        deal(nc.vector.tensor_copy, w1_g, w1_hi, H // 2, H // 2, H)
        w1_c = tile("w1_c", [P, H], U32)
        w1_s = tile("w1_s", [P, H], U8)
        for c0, c1 in ((0, P), (P, H)):
            nc.vector.quantize_mx(out=w1_c[:, c0:c1].bitcast(FP8X4), scales=w1_s[:, c0:c1], in_=w1_g[:, PACK * c0 : PACK * c1])
        lam25 = late.tile([P, PACK, V], F32, name="lam25", offset=Z, align_bytes=64)
        nc.vector.tensor_scalar(lam25[:], lam_t[:], 2.5, None, ALU.mult)
        es = late.tile([P, Z], U8, name="es", offset=0, align_bytes=64)
        nc.vector.tensor_copy(es[:], es_tab[:].indirect(prt_t[:]))
        u_min = tile("u_min", [P, PACK], F32)
        u_b = tile("u_b", [P, PACK], F32)
        nc.gpsimd.tensor_scalar(u_min[:], unit_t[:], -0.4, 0.0, ALU.mult, ALU.add)
        nc.gpsimd.tensor_scalar(u_b[:], unit_t[:], 0.6, 0.0, ALU.mult, ALU.add)

        yv = [shared.tile([P, S], F32, name="yv%d" % t, offset=t * S * 4) for t in range(PACK)]
        y = [tile("y%d" % t, [P, S], F32) for t in range(PACK)]
        b = [tile("b%d" % t, [P, V], F32) for t in range(PACK)]
        d = [tile("es_tab", [P, V], F32), tile("d1", [P, V], F32)]
        a = {t: tile("a%d" % t, [P, V], F32) for t in (2, 3)}
        coef = [tile("coef%d" % t, [P, V], F32) for t in range(PACK)]
        term = [tile("term%d" % t, [P, V], F32) for t in range(PACK)]
        hid = tile("hid", [P, PACK, V], F32)

        def fetch_b(t):
            nc.scalar.activation(b[t][:], yv[t][:].indirect(crb_t[:]), ACT.Copy)

        def fetch_a(t):
            nc.scalar.activation(a[t][:], y[t][:].indirect(cra_t[:]), ACT.Copy)

        acc_v = [product(t, w2_c, w2_s, P * t, xw, xs) for t in range(2)]
        acc_y = [product(2 + t, w1_c, w1_s, P * t, xw, xs) for t in range(PACK)]
        for t in range(2):
            nc.scalar.copy(yv[t][:], acc_v[t][:])
        for t in range(2):
            fetch_b(t)
            nc.scalar.copy(y[t][:], acc_y[t][:])
        for t in range(2, PACK):
            nc.scalar.copy(yv[t][:], product(t, w2_c, w2_s, P * t, xw, xs)[:])
            nc.scalar.copy(y[t][:], acc_y[t][:])
            fetch_b(t)
            fetch_a(t)

        def share(t, v0, v1):
            nc.vector.scalar_tensor_tensor(coef[t][:, v0:v1], d[t][:, v0:v1], 0.0, lam25[:, t, v0:v1], ALU.is_lt, ALU.subtract)

        def scale(t, v0, v1):
            nc.vector.scalar_tensor_tensor(term[t][:, v0:v1], coef[t][:, v0:v1], u_min[:, t : t + 1], d[t][:, v0:v1], ALU.mult, ALU.mult)

        def join(t, v0, v1):
            nc.vector.scalar_tensor_tensor(hid[:, t, v0:v1], b[t][:, v0:v1], u_b[:, t : t + 1], term[t][:, v0:v1], ALU.mult, ALU.add)

        for t in range(2):
            nc.vector.tensor_tensor(d[t][:], y[t][:].indirect(cra_t[:]), b[t][:], ALU.subtract)
        share(0, 0, V)
        share(1, 0, V)
        ew = gather("y1", ew_tab, prt_t, Z, U32)
        scale(0, 0, V)
        scale(1, 0, V)
        join(0, 0, V)
        d.append(tile("ew_tab", [P, V], F32))
        nc.vector.tensor_tensor(d[2][:], a[2][:], b[2][:], ALU.subtract)
        join(1, 0, V)
        share(2, 0, V)
        d.append(tile("term0", [P, V], F32))
        nc.vector.tensor_tensor(d[3][:], a[3][:], b[3][:], ALU.subtract)
        scale(2, 0, V)
        share(3, 0, V)
        join(2, 0, V)
        for step in (scale, join):
            for v0 in range(0, V, P):
                step(3, v0, v0 + P)

        temp = tile("y3", [P, Z], F32)
        nc.scalar.activation(temp[:], tmp_tab[:].indirect(prt_t[:]), ACT.Copy)

        halves = range(V // P)
        hid_g = [tile("hid_g%d" % h, [P, P, PACK], BF16) for h in halves]
        hid_c = [tile("hid_c%d" % h, [P, P], U32) for h in halves]
        hid_s = [tile("hid_s%d" % h, [P, P], U8) for h in halves]
        for h, copy in zip(halves, (nc.vector.tensor_copy, nc.scalar.copy)):
            copy(out=hid_g[h][:], in_=hid[:, :, P * h : P * (h + 1)].rearrange("p t v -> p v t"))
        acc_s = []
        for h in halves:
            nc.vector.quantize_mx(out=hid_c[h][:].bitcast(FP8X4), scales=hid_s[h][:], in_=hid_g[h][:].rearrange("p v t -> p (v t)"))
            acc_s.append(product(6 + h, hid_c[h], hid_s[h], 0, ew, es))

        part = [tile("part%d" % h, [P, Z], F32) for h in halves]
        mu = [tile("mu%d" % h, [P, 1], F32) for h in halves]
        mu_part = [tile("mu_part%d" % h, [P, 1], F32) for h in halves]
        sq = [tile("sq%d" % h, [P, Z], F32) for h in halves]
        ssq = [tile("ssq%d" % h, [P, 1], F32) for h in halves]
        inv = [tile("inv%d" % h, [P, 1], F32) for h in halves]
        res = [tile("res%d" % h, [P, Z], F32) for h in halves]
        for h in halves:
            nc.vector.scalar_tensor_tensor(part[h][:], acc_s[h][:], 1.0 / Z, temp[:], ALU.mult, ALU.mult, accum_out=mu[h][:])
            nc.scalar.activation(sq[h][:], part[h][:], ACT.Square, bias=mu[h][:], scale=-float(Z), accum_out=ssq[h][:])
        for h in halves:
            nc.scalar.activation(inv[h][:], ssq[h][:], ACT.Abs_reciprocal_sqrt, bias=EPS / Z**2, scale=1.0 / Z**3)
        for h in halves:
            nc.vector.tensor_scalar(mu_part[h][:], mu[h][:], 1.0 / Z, None, ALU.mult)
        for h in halves:
            nc.vector.tensor_scalar(res[h][:], part[h][:], mu_part[h][:], inv[h][:], ALU.subtract, ALU.mult)
            nc.sync.dma_start(out[P * h : P * (h + 1), :], res[h][:])
